import numpy as np
import ml_dtypes


def mxq(x, axis, fmt="e4m3"):
    dtype, down = {"e4m3": (ml_dtypes.float8_e4m3fn, 7), "e5m2": (ml_dtypes.float8_e5m2, 14)}[fmt]
    v = np.moveaxis(np.asarray(x, np.float32).astype(ml_dtypes.bfloat16).astype(np.float64), axis, -1)
    blocks = v.reshape(v.shape[:-1] + (-1, 32))
    amax = np.abs(blocks).max(-1, keepdims=True)
    byte = np.maximum(np.where(amax > 0, np.frexp(amax)[1] - 1 + 127, 0) - down, 1)
    scale = np.exp2(byte - 127.0)
    codes = (blocks / scale).astype(np.float32).astype(dtype).astype(np.float64)
    return np.moveaxis((codes * scale).reshape(v.shape), -1, axis)


WIDE = False


def mx_kscale(k):
    if not WIDE:
        return np.ones(k)
    levels = np.array([10, -10, 5, -5, 0])
    if k % 512:
        return np.exp2(np.random.permutation(np.resize(levels, k // 32))).repeat(32)
    a = np.empty((k // 512, 16))
    for p in range(k // 512):
        a[p, :8] = np.random.permutation(np.resize(levels, 8))
        for g in range(8):
            far = levels[np.abs(levels - a[p, g]) >= 10]
            a[p, g + 8] = far[np.random.randint(len(far))]
    return np.exp2(a.ravel()).repeat(32)


def f64(x):
    return np.asarray(x).astype(np.float64)


def striped(idx):
    return np.tile(np.asarray(idx).reshape(-1, 16).T, (8, 1)).astype(np.uint16)


def unstriped(offs):
    return offs[:16].T.reshape(-1).astype(np.int64)


E2M1 = np.array([0.0, 0.5, 1.0, 1.5, 2.0, 3.0, 4.0, 6.0, -0.0, -0.5, -1.0, -1.5, -2.0, -3.0, -4.0, -6.0])


def pack_weight(w, fmt):
    k, n = w.shape
    w = f64(np.asarray(w, np.float32).astype(ml_dtypes.bfloat16)).reshape(k // 32, 32, n)
    amax = np.abs(w).max(1)
    if fmt == "e4m3":
        byte = np.frexp(amax)[1] - 1 + 127 - 7
    else:
        mant, ex = np.frexp(amax / 6.0)
        byte = np.where(mant > 0.5, ex, ex - 1) + 127
    byte = np.clip(np.where(amax > 0, byte, 1), 1, 254)
    scaled = (w * np.exp2(127.0 - byte)[:, None, :]).reshape(k, n).astype(np.float32)
    by_word = np.ascontiguousarray(scaled.reshape(k // 512, 128, 4, n).transpose(0, 1, 3, 2))
    if fmt == "e4m3":
        words = by_word.astype(ml_dtypes.float8_e4m3fn).view(np.uint8)
    else:
        c = by_word.astype(ml_dtypes.float4_e2m1fn).view(np.uint8) & 0xF
        words = (c[..., 0::2] | (c[..., 1::2] << 4)).reshape(k // 512, 128, 2 * n)
    return np.ascontiguousarray(words), np.ascontiguousarray(byte.astype(np.uint8).reshape(k // 512, 16, n))


def unpack_weight(words, scales, fmt):
    g, _, n = scales.shape
    words = np.ascontiguousarray(words).reshape(g, 128, n, -1)
    if fmt == "e4m3":
        vals = words.view(ml_dtypes.float8_e4m3fn).astype(np.float64)
    else:
        nib = np.empty((g, 128, n, 4), np.uint8)
        nib[..., 0::2] = words & 0xF
        nib[..., 1::2] = words >> 4
        vals = E2M1[nib]
    vals = vals * np.repeat(np.exp2(scales.astype(np.float64) - 127.0), 8, axis=1)[..., None]
    return vals.transpose(0, 1, 3, 2).reshape(g * 512, n)


D, T, I, J, U, X, Z, E = 512, 2048, 512, 512, 1024, 1024, 1024, 512


def setup_inputs():
    n = np.random.standard_normal
    idx = np.random.permutation(T)[:I]
    idx2 = np.random.permutation(U)[:J]
    idx3 = np.random.permutation(X)[:I]
    idx4 = np.random.permutation(Z)[:J]
    fd = mx_kscale(D)
    fi = mx_kscale(I)
    ti = np.ones(T)
    ti[idx] = fi
    keysp = pack_weight(n((D, T)) / fd[:, None], "e4m3")
    morep = pack_weight(n((D, X)) / fd[:, None], "e4m3")
    return {
        "keys_words": keysp[0],
        "keys_scales": keysp[1],
        "notes": (n((D, U)) * 1.0 / np.sqrt(D) * fd[:, None]).astype(np.float32),
        "more_words": morep[0],
        "more_scales": morep[1],
        "users2": (n((D, Z)) * 1.0 / np.sqrt(D) * fd[:, None]).astype(np.float32),
        "rowf": (np.random.uniform(0.02, 0.08, (I, 1)) * fi[:, None]).astype(np.float32),
        "vals": (n((E, T)) / ti).astype(np.float32),
        "mem": (np.random.uniform(0.3, 1.0, (1, J))).astype(np.float32),
        "offs": striped(idx),
        "offs2": striped(idx2),
        "offs3": striped(idx3),
        "offs4": striped(idx4),
    }


def reference(keys_words, keys_scales, notes, more_words, more_scales, users2, rowf, vals, mem, offs, offs2, offs3, offs4):
    idx = unstriped(offs)
    idx2 = unstriped(offs2)
    idx3 = unstriped(offs3)
    idx4 = unstriped(offs4)
    keysu = unpack_weight(keys_words, keys_scales, "e4m3")
    moreu = unpack_weight(more_words, more_scales, "e4m3")
    keysidxg = keysu[:, idx]
    notesidx2q = mxq(f64(notes)[:, idx2], 0, "e4m3")
    moreidx3g = moreu[:, idx3]
    users2idx4q = mxq(f64(users2)[:, idx4], 0, "e4m3")
    g9 = keysidxg.T @ notesidx2q + moreidx3g.T @ users2idx4q
    g0 = np.maximum(g9, 0.0)
    gr1 = g0 * f64(rowf)
    vt1 = f64(vals)[:, idx].T
    vt1q = mxq(vt1, 0, "e4m3")
    gr1q = mxq(gr1, 0, "e4m3")
    o = vt1q.T @ gr1q
    o1 = np.pad(o, ((0, 0), (1, 0)))[:, :J]
    y = o - o1 * f64(mem)
    return y

@@ -1,0 +1,203 @@
+from contextlib import ExitStack
+
+import concourse.mybir as mybir
+from concourse.masks import make_identity
+
+F32 = mybir.dt.float32
+BF16 = mybir.dt.bfloat16
+I32 = mybir.dt.int32
+U32 = mybir.dt.uint32
+U16 = mybir.dt.uint16
+U8 = mybir.dt.uint8
+FP8X4 = mybir.dt.float8_e4m3fn_x4
+ALU = mybir.AluOpType
+COPY = mybir.ActivationFunctionType.Copy
+
+P = 128
+D, T, I, J, U, X, Z, E = 512, 2048, 512, 512, 1024, 1024, 1024, 512
+FLOPS = 2 * (2 * D * I * J + I * E * J)
+
+
+def tile_attend_tab_twosum_changes_kernel(tc, keys_words, keys_scales, notes, more_words, more_scales, users2,
+                                           rowf, vals, mem, offs, offs2, offs3, offs4, out):
+    nc = tc.nc
+    with ExitStack() as ctx:
+        lists = ctx.enter_context(tc.tile_pool(name="lists", bufs=1))
+        keep = ctx.enter_context(tc.tile_pool(name="keep", bufs=1))
+        psum = ctx.enter_context(tc.psum_pool(name="psum", bufs=1))
+
+        def sb(shape, dtype, name):
+            return keep.tile(shape, dtype, name=name, align_bytes=64)
+
+        def load_list(src, name):
+            t = lists.tile([P, 32], U16, name=name)
+            nc.sync.dma_start(t[:], src)
+            return t
+
+        def load_plane(src, t, name):
+            w = sb([P, src.shape[1]], F32, name)
+            nc.sync.dma_start(w[:], src.rearrange("(p t) u -> t p u", t=4)[t])
+            return w
+
+        def load_words(src, name):
+            w = sb([P, src.shape[2]], I32, name)
+            nc.sync.dma_start(w[:], src[0].rearrange("p n t -> p (n t)").bitcast(I32))
+            return w
+
+        def clear_scales(src, name):
+            w = sb([P, src.shape[2]], U8, name)
+            nc.vector.memset(w[:].bitcast(I32), 0)
+            return w
+
+        def load_scales(w, src, q, k):
+            nc.sync.dma_start(w[32 * q + k : 32 * q + k + 4, :].bitcast(I32), src[0, 4 * q : 4 * q + 4, :].bitcast(I32))
+
+        def load_vals(b):
+            w = sb([P, T], F32, "vals%d" % b)
+            nc.sync.dma_start(w[:], vals[P * b : P * (b + 1), :])
+            return w
+
+        ks_win = clear_scales(keys_scales, "ks_win")
+        ms_win = clear_scales(more_scales, "ms_win")
+        rowf_sb = sb([P, 4], F32, "rowf_sb")
+        mem_col = sb([P, 4], F32, "mem_col")
+        ident = sb([P, P], F32, "ident")
+        make_identity(nc, ident[:])
+        shifted = sb([P, 4, J], F32, "shifted")
+        nc.vector.memset(shifted[:, :, 0:1], 0.0)
+
+        l2 = load_list(offs2, "l2")
+        n_win = [load_plane(notes, t, "n%d" % t) for t in range(2)]
+        l1 = load_list(offs, "l1")
+        load_scales(ks_win, keys_scales, 0, 0)
+        load_scales(ks_win, keys_scales, 1, 0)
+        n_win += [load_plane(notes, t, "n%d" % t) for t in range(2, 4)]
+        load_scales(ks_win, keys_scales, 2, 0)
+        load_scales(ks_win, keys_scales, 3, 0)
+        l4 = load_list(offs4, "l4")
+        u_win = [load_plane(users2, 0, "u0")]
+        l3 = load_list(offs3, "l3")
+        u_win.append(load_plane(users2, 1, "u1"))
+        for q in range(4):
+            load_scales(ms_win, more_scales, q, 4)
+        u_win += [load_plane(users2, t, "u%d" % t) for t in range(2, 4)]
+        mw_win = load_words(more_words, "mw_win")
+        kw_win = load_words(keys_words, "kw_win")
+        nc.sync.dma_start(rowf_sb[:], rowf.rearrange("(p r) o -> p (r o)", r=4))
+        v_win = [load_vals(0)]
+        nc.sync.dma_start(mem_col[:], mem.rearrange("o (k c) -> (o k) c", c=4))
+        v_win += [load_vals(b) for b in range(1, 4)]
+
+        def gather_float(engine, dst, win, lst):
+            if engine == "v":
+                nc.vector.tensor_copy(dst, win[:].indirect(lst))
+            else:
+                nc.scalar.activation(dst, win[:].indirect(lst), COPY)
+
+        def dealt(t):
+            return t[:].rearrange("p r s -> p s r")
+
+        def gather_words(win, lst, name):
+            g = sb([P, 4, P], U32, name)
+            nc.vector.tensor_copy(dealt(g), win[:].bitcast(U32).indirect(lst[:]))
+            return g
+
+        def gather_scales(win, lst, name):
+            g = sb([P, 4, P], U8, name)
+            nc.vector.tensor_copy(dealt(g), win[:].indirect(lst[:]))
+            return g
+
+        def interleave(planes, name):
+            g = sb([P, J, 4], BF16, name)
+            nc.vector.tensor_copy(g[:].rearrange("p (c i) t -> p c t i", i=4), planes[:].rearrange("p t (c i) -> p c t i", i=4))
+            return g
+
+        def quantize(g, width, name):
+            codes = sb([P, width], U32, name + "_codes")
+            scales = sb([P, width], U8, name + "_scales")
+            nc.vector.quantize_mx(out=codes[:].bitcast(FP8X4), scales=scales[:], in_=g[:].rearrange("p w t -> p (w t)"))
+            return codes, scales
+
+        n_planes = sb([P, 4, J], BF16, "n_planes")
+        u_planes = sb([P, 4, J], BF16, "u_planes")
+        banks = [psum.tile([P, 4, P], F32, name="table%d" % c) for c in range(4)]
+
+        def table_passes(words, scales, k, codes, cscales, first):
+            for c in range(4):
+                cols = slice(P * c, P * (c + 1))
+                for r in range(4):
+                    nc.tensor.matmul_mx(out=banks[c][:, r, :], lhsT=words[:, r, :].bitcast(FP8X4), lhsT_scale=scales[k:P, r, :],
+                                        rhs=codes[:, cols].bitcast(FP8X4), rhs_scale=cscales[:, cols],
+                                        start=(first and r == 0), stop=(not first and r == 3))
+
+        mem_row = sb([P, J], F32, "mem_row")
+
+        def spread_mem():
+            bank = psum.tile([P, 4, P], F32, name="turn", bufs=2)
+            for c in range(4):
+                nc.tensor.transpose(bank[:, c, :], mem_col[:, c : c + 1].to_broadcast([P, P]), ident[:])
+            nc.scalar.copy(mem_row[:].rearrange("p (k c) -> p k c", c=4), bank[:].rearrange("p c k -> p k c"))
+
+        gr = sb([P, J, 4], BF16, "gr")
+        gr_codes = sb([P, J], U32, "gr_codes")
+        gr_scales = sb([P, J], U8, "gr_scales")
+        rowf_b = rowf_sb[:].rearrange("p (o r) -> p o r", o=1).to_broadcast([P, P, 4])
+
+        def table_out(c):
+            nc.vector.scalar_tensor_tensor(gr[:, P * c : P * (c + 1), :], banks[c][:].rearrange("p r n -> p n r"), 0.0, rowf_b, ALU.max, ALU.mult)
+
+        def table_quant(c0, c1):
+            cols = slice(P * c0, P * c1)
+            nc.vector.quantize_mx(out=gr_codes[:, cols].bitcast(FP8X4), scales=gr_scales[:, cols], in_=gr[:, cols, :].rearrange("p w t -> p (w t)"))
+
+        def vals_gather(b, split):
+            g = sb([P, I], BF16, "vg%d" % b)
+            if split:
+                gather_float("s", g[:, 0:split], v_win[b], l1[:, 0 : split // 16])
+                gather_float("v", g[:, split:I], v_win[b], l1[:, split // 16 : I // 16])
+            else:
+                gather_float("s", g[:], v_win[b], l1[:])
+            return g
+
+        def vals_turn(b, g):
+            words = g[:].bitcast(F32)
+            bank = psum.tile([P, 4, P], F32, name="turn", bufs=2)
+            for u in range(2):
+                nc.tensor.transpose(bank[:, u, :], words[:, u : 2 * P : 2], ident[:])
+            vt = sb([P, P, 4], BF16, "vt%d" % b)
+            nc.scalar.copy(vt[:].bitcast(F32), bank[:, 0:2, :].rearrange("p u e -> p e u"))
+            return vt
+
+        def product(b, vq):
+            o = psum.tile([P, J], F32, name="o", bufs=2)
+            nc.tensor.matmul_mx(out=o[:], lhsT=vq[0][:].bitcast(FP8X4), lhsT_scale=vq[1][:], rhs=gr_codes[:].bitcast(FP8X4), rhs_scale=gr_scales[:], start=True, stop=True)
+            return o
+
+        def finish(b, o):
+            nc.vector.tensor_tensor(shifted[:, b, 1:J], o[:, 0 : J - 1], mem_row[:, 1:J], ALU.mult)
+            res = sb([P, J], F32, "res%d" % b)
+            nc.vector.tensor_tensor(res[:], o[:], shifted[:, b, :], ALU.subtract)
+            nc.sync.dma_start(out[P * b : P * (b + 1), :], res[:])
+
+        for t in range(4):
+            gather_float("sv"[t % 2], n_planes[:, t, :], n_win[t], l2[:])
+        nq = quantize(interleave(n_planes, "n_grp"), J, "n")
+        for t in range(4):
+            gather_float("s", u_planes[:, t, :], u_win[t], l4[:])
+        ks = gather_scales(ks_win, l1, "ks")
+        ms = gather_scales(ms_win, l3, "ms")
+        mw = gather_words(mw_win, l3, "mw")
+        uq = quantize(interleave(u_planes, "u_grp"), J, "u")
+        spread_mem()
+        table_passes(mw, ms, 4, uq[0], uq[1], True)
+        kw = gather_words(kw_win, l1, "kw")
+        table_passes(kw, ks, 0, nq[0], nq[1], False)
+        for c in range(3):
+            table_out(c)
+        table_quant(0, 2)
+        table_out(3)
+        table_quant(2, 4)
+        for b in range(4):
+            g = vals_gather(b, 256 if b == 3 else 0)
+            vq = quantize(vals_turn(b, g), P, "v%d" % b)
+            finish(b, product(b, vq))

@@ -26,8 +26,8 @@ def tile_attend_tab_twosum_changes_kernel(tc, keys_words, keys_scales, notes, mo
         keep = ctx.enter_context(tc.tile_pool(name="keep", bufs=1))
         psum = ctx.enter_context(tc.psum_pool(name="psum", bufs=1))
 
-        def sb(shape, dtype, name):
-            return keep.tile(shape, dtype, name=name, align_bytes=64)
+        def sb(shape, dtype, name, tag=None):
+            return keep.tile(shape, dtype, name=name, tag=tag or name, align_bytes=64)
 
         def load_list(src, name):
             t = lists.tile([P, 32], U16, name=name)
@@ -44,9 +44,9 @@ def tile_attend_tab_twosum_changes_kernel(tc, keys_words, keys_scales, notes, mo
             nc.sync.dma_start(w[:], src[0].rearrange("p n t -> p (n t)").bitcast(I32))
             return w
 
-        def clear_scales(src, name):
+        def clear_scales(engine, src, name):
             w = sb([P, src.shape[2]], U8, name)
-            nc.vector.memset(w[:].bitcast(I32), 0)
+            engine.memset(w[:].bitcast(I32), 0)
             return w
 
         def load_scales(w, src, q, k):
@@ -57,8 +57,8 @@ def tile_attend_tab_twosum_changes_kernel(tc, keys_words, keys_scales, notes, mo
             nc.sync.dma_start(w[:], vals[P * b : P * (b + 1), :])
             return w
 
-        ks_win = clear_scales(keys_scales, "ks_win")
-        ms_win = clear_scales(more_scales, "ms_win")
+        ms_win = clear_scales(nc.gpsimd, more_scales, "ms_win")
+        ks_win = clear_scales(nc.vector, keys_scales, "ks_win")
         rowf_sb = sb([P, 4], F32, "rowf_sb")
         mem_col = sb([P, 4], F32, "mem_col")
         ident = sb([P, P], F32, "ident")
@@ -66,27 +66,28 @@ def tile_attend_tab_twosum_changes_kernel(tc, keys_words, keys_scales, notes, mo
         shifted = sb([P, 4, J], F32, "shifted")
         nc.vector.memset(shifted[:, :, 0:1], 0.0)
 
-        l2 = load_list(offs2, "l2")
-        n_win = [load_plane(notes, t, "n%d" % t) for t in range(2)]
-        l1 = load_list(offs, "l1")
-        load_scales(ks_win, keys_scales, 0, 0)
-        load_scales(ks_win, keys_scales, 1, 0)
-        n_win += [load_plane(notes, t, "n%d" % t) for t in range(2, 4)]
-        load_scales(ks_win, keys_scales, 2, 0)
-        load_scales(ks_win, keys_scales, 3, 0)
+        l3 = load_list(offs3, "l3")
+        mw_win = load_words(more_words, "mw_win")
         l4 = load_list(offs4, "l4")
         u_win = [load_plane(users2, 0, "u0")]
-        l3 = load_list(offs3, "l3")
-        u_win.append(load_plane(users2, 1, "u1"))
-        for q in range(4):
-            load_scales(ms_win, more_scales, q, 4)
-        u_win += [load_plane(users2, t, "u%d" % t) for t in range(2, 4)]
-        mw_win = load_words(more_words, "mw_win")
-        kw_win = load_words(keys_words, "kw_win")
-        nc.sync.dma_start(rowf_sb[:], rowf.rearrange("(p r) o -> p (r o)", r=4))
-        v_win = [load_vals(0)]
         nc.sync.dma_start(mem_col[:], mem.rearrange("o (k c) -> (o k) c", c=4))
-        v_win += [load_vals(b) for b in range(1, 4)]
+        u_win.append(load_plane(users2, 1, "u1"))
+        l1 = load_list(offs, "l1")
+        u_win.append(load_plane(users2, 2, "u2"))
+        for q in range(4):
+            load_scales(ks_win, keys_scales, q, 0)
+        u_win.append(load_plane(users2, 3, "u3"))
+        l2 = load_list(offs2, "l2")
+        n_win = [load_plane(notes, 0, "n0")]
+        load_scales(ms_win, more_scales, 0, 4)
+        load_scales(ms_win, more_scales, 1, 4)
+        n_win.append(load_plane(notes, 1, "n1"))
+        load_scales(ms_win, more_scales, 2, 4)
+        load_scales(ms_win, more_scales, 3, 4)
+        n_win += [load_plane(notes, t, "n%d" % t) for t in range(2, 4)]
+        nc.sync.dma_start(rowf_sb[:], rowf.rearrange("(p r) o -> p (r o)", r=4))
+        kw_win = load_words(keys_words, "kw_win")
+        v_win = [load_vals(b) for b in range(4)]
 
         def gather_float(engine, dst, win, lst):
             if engine == "v":
@@ -107,24 +108,23 @@ def tile_attend_tab_twosum_changes_kernel(tc, keys_words, keys_scales, notes, mo
             nc.vector.tensor_copy(dealt(g), win[:].indirect(lst[:]))
             return g
 
-        def interleave(planes, name):
-            g = sb([P, J, 4], BF16, name)
-            nc.vector.tensor_copy(g[:].rearrange("p (c i) t -> p c t i", i=4), planes[:].rearrange("p t (c i) -> p c t i", i=4))
-            return g
+        def weave(copy, g, planes, c0, c1):
+            copy(g[:, c0:c1, :].rearrange("p (c i) t -> p c t i", i=4), planes[:, :, c0:c1].rearrange("p t (c i) -> p c t i", i=4))
 
-        def quantize(g, width, name):
-            codes = sb([P, width], U32, name + "_codes")
-            scales = sb([P, width], U8, name + "_scales")
-            nc.vector.quantize_mx(out=codes[:].bitcast(FP8X4), scales=scales[:], in_=g[:].rearrange("p w t -> p (w t)"))
+        def quantize(g, c0, c1, name, tag=None):
+            codes = sb([P, c1 - c0], U32, name + "_codes", tag)
+            scales = sb([P, c1 - c0], U8, name + "_scales")
+            nc.vector.quantize_mx(out=codes[:].bitcast(FP8X4), scales=scales[:], in_=g[:, c0:c1, :].rearrange("p w t -> p (w t)"))
             return codes, scales
 
         n_planes = sb([P, 4, J], BF16, "n_planes")
         u_planes = sb([P, 4, J], BF16, "u_planes")
         banks = [psum.tile([P, 4, P], F32, name="table%d" % c) for c in range(4)]
 
-        def table_passes(words, scales, k, codes, cscales, first):
+        def table_passes(words, scales, k, halves, first):
             for c in range(4):
-                cols = slice(P * c, P * (c + 1))
+                codes, cscales = halves[c // 2]
+                cols = slice(P * (c % 2), P * (c % 2 + 1))
                 for r in range(4):
                     nc.tensor.matmul_mx(out=banks[c][:, r, :], lhsT=words[:, r, :].bitcast(FP8X4), lhsT_scale=scales[k:P, r, :],
                                         rhs=codes[:, cols].bitcast(FP8X4), rhs_scale=cscales[:, cols],
@@ -133,7 +133,7 @@ def tile_attend_tab_twosum_changes_kernel(tc, keys_words, keys_scales, notes, mo
         mem_row = sb([P, J], F32, "mem_row")
 
         def spread_mem():
-            bank = psum.tile([P, 4, P], F32, name="turn", bufs=2)
+            bank = psum.tile([P, 4, P], F32, name="turn", bufs=4)
             for c in range(4):
                 nc.tensor.transpose(bank[:, c, :], mem_col[:, c : c + 1].to_broadcast([P, P]), ident[:])
             nc.scalar.copy(mem_row[:].rearrange("p (k c) -> p k c", c=4), bank[:].rearrange("p c k -> p k c"))
@@ -161,43 +161,75 @@ def tile_attend_tab_twosum_changes_kernel(tc, keys_words, keys_scales, notes, mo
 
         def vals_turn(b, g):
             words = g[:].bitcast(F32)
-            bank = psum.tile([P, 4, P], F32, name="turn", bufs=2)
+            bank = psum.tile([P, 4, P], F32, name="turn", bufs=4)
             for u in range(2):
                 nc.tensor.transpose(bank[:, u, :], words[:, u : 2 * P : 2], ident[:])
-            vt = sb([P, P, 4], BF16, "vt%d" % b)
+            vt = sb([P, P, 4], BF16, "vt%d" % b, "vals1" if b == 0 else None)
             nc.scalar.copy(vt[:].bitcast(F32), bank[:, 0:2, :].rearrange("p u e -> p e u"))
             return vt
 
         def product(b, vq):
-            o = psum.tile([P, J], F32, name="o", bufs=2)
+            o = psum.tile([P, J], F32, name="table%d" % b)
             nc.tensor.matmul_mx(out=o[:], lhsT=vq[0][:].bitcast(FP8X4), lhsT_scale=vq[1][:], rhs=gr_codes[:].bitcast(FP8X4), rhs_scale=gr_scales[:], start=True, stop=True)
             return o
 
-        def finish(b, o):
+        def shift(b, o):
             nc.vector.tensor_tensor(shifted[:, b, 1:J], o[:, 0 : J - 1], mem_row[:, 1:J], ALU.mult)
-            res = sb([P, J], F32, "res%d" % b)
+
+        def finish(b, o):
+            res = sb([P, J], F32, "res%d" % b, {0: "vt2", 2: "vt3"}.get(b))
             nc.vector.tensor_tensor(res[:], o[:], shifted[:, b, :], ALU.subtract)
             nc.sync.dma_start(out[P * b : P * (b + 1), :], res[:])
 
-        for t in range(4):
-            gather_float("sv"[t % 2], n_planes[:, t, :], n_win[t], l2[:])
-        nq = quantize(interleave(n_planes, "n_grp"), J, "n")
-        for t in range(4):
-            gather_float("s", u_planes[:, t, :], u_win[t], l4[:])
-        ks = gather_scales(ks_win, l1, "ks")
-        ms = gather_scales(ms_win, l3, "ms")
+        def last_block(b, vq):
+            H = J // 2
+            o = [psum.tile([P, H], F32, name="table3"), psum.tile([P, H], F32, name="turn", bufs=4)]
+            for h in range(2):
+                cols = slice(H * h, H * (h + 1))
+                nc.tensor.matmul_mx(out=o[h][:], lhsT=vq[0][:].bitcast(FP8X4), lhsT_scale=vq[1][:], rhs=gr_codes[:, cols].bitcast(FP8X4), rhs_scale=gr_scales[:, cols], start=True, stop=True)
+            nc.vector.tensor_tensor(shifted[:, b, 1 : H + 1], o[0][:], mem_row[:, 1 : H + 1], ALU.mult)
+            nc.vector.tensor_tensor(shifted[:, b, H + 1 : J], o[1][:, 0 : H - 1], mem_row[:, H + 1 : J], ALU.mult)
+            for h in range(2):
+                cols = slice(H * h, H * (h + 1))
+                res = sb([P, H], F32, "last%d" % h)
+                nc.vector.tensor_tensor(res[:], o[h][:], shifted[:, b, cols], ALU.subtract)
+                nc.sync.dma_start(out[P * b : P * (b + 1), cols], res[:])
+
         mw = gather_words(mw_win, l3, "mw")
-        uq = quantize(interleave(u_planes, "u_grp"), J, "u")
+        gather_float("s", u_planes[:, 0, :], u_win[0], l4[:])
         spread_mem()
-        table_passes(mw, ms, 4, uq[0], uq[1], True)
+        gather_float("v", u_planes[:, 1, :], u_win[1], l4[:])
+        gather_float("s", u_planes[:, 2, :], u_win[2], l4[:])
+        ks = gather_scales(ks_win, l1, "ks")
+        gather_float("v", u_planes[:, 3, :], u_win[3], l4[:])
+        u_grp = sb([P, J, 4], BF16, "u_grp")
+        weave(nc.vector.tensor_copy, u_grp, u_planes, 0, J)
+        uq = quantize(u_grp, 0, J, "u")
+        ms = gather_scales(ms_win, l3, "ms")
+        table_passes(mw, ms, 4, [(uq[0][:, 0:256], uq[1][:, 0:256]), (uq[0][:, 256:512], uq[1][:, 256:512])], True)
+        for t in range(3):
+            gather_float("s", n_planes[:, t, :], n_win[t], l2[:])
+        gather_float("s", n_planes[:, 3, 0:256], n_win[3], l2[:, 0:16])
+        gather_float("v", n_planes[:, 3, 256:512], n_win[3], l2[:, 16:32])
+        n_grp = sb([P, J, 4], BF16, "n_grp")
+        weave(nc.vector.tensor_copy, n_grp, n_planes, 0, 352)
+        weave(nc.scalar.copy, n_grp, n_planes, 352, J)
+        nq0 = quantize(n_grp, 0, 256, "na")
         kw = gather_words(kw_win, l1, "kw")
-        table_passes(kw, ks, 0, nq[0], nq[1], False)
+        nq1 = quantize(n_grp, 256, J, "nb", "kw_win")
+        table_passes(kw, ks, 0, [nq0, nq1], False)
+        vg = [vals_gather(b, 0) for b in range(4)]
         for c in range(3):
             table_out(c)
         table_quant(0, 2)
         table_out(3)
         table_quant(2, 4)
-        for b in range(4):
-            g = vals_gather(b, 256 if b == 3 else 0)
-            vq = quantize(vals_turn(b, g), P, "v%d" % b)
-            finish(b, product(b, vq))
+        vq = [quantize(vals_turn(b, vg[b]), 0, P, "v%d" % b) for b in range(4)]
+        prods = [product(b, vq[b]) for b in range(3)]
+        shift(0, prods[0])
+        shift(1, prods[1])
+        finish(0, prods[0])
+        finish(1, prods[1])
+        shift(2, prods[2])
+        finish(2, prods[2])
+        last_block(3, vq[3])

@@ -50,15 +50,15 @@ def tile_attend_tab_twosum_changes_kernel(tc, keys_words, keys_scales, notes, mo
             return w
 
         def load_scales(w, src, q, k):
-            nc.sync.dma_start(w[32 * q + k : 32 * q + k + 4, :].bitcast(I32), src[0, 4 * q : 4 * q + 4, :].bitcast(I32))
+            nc.sync.dma_start(w[k + q : P : 32, :].bitcast(I32), src[0, q : 16 : 4, :].bitcast(I32))
 
         def load_vals(b):
             w = sb([P, T], F32, "vals%d" % b)
             nc.sync.dma_start(w[:], vals[P * b : P * (b + 1), :])
             return w
 
-        ms_win = clear_scales(nc.gpsimd, more_scales, "ms_win")
-        ks_win = clear_scales(nc.vector, keys_scales, "ks_win")
+        ms_win = clear_scales(nc.vector, more_scales, "ms_win")
+        ks_win = clear_scales(nc.gpsimd, keys_scales, "ks_win")
         rowf_sb = sb([P, 4], F32, "rowf_sb")
         mem_col = sb([P, 4], F32, "mem_col")
         ident = sb([P, P], F32, "ident")
@@ -66,11 +66,12 @@ def tile_attend_tab_twosum_changes_kernel(tc, keys_words, keys_scales, notes, mo
         shifted = sb([P, 4, J], F32, "shifted")
         nc.vector.memset(shifted[:, :, 0:1], 0.0)
 
-        l3 = load_list(offs3, "l3")
         mw_win = load_words(more_words, "mw_win")
-        l4 = load_list(offs4, "l4")
+        l3 = load_list(offs3, "l3")
         u_win = [load_plane(users2, 0, "u0")]
-        nc.sync.dma_start(mem_col[:], mem.rearrange("o (k c) -> (o k) c", c=4))
+        l4 = load_list(offs4, "l4")
+        for q in range(4):
+            load_scales(ms_win, more_scales, q, 4)
         u_win.append(load_plane(users2, 1, "u1"))
         l1 = load_list(offs, "l1")
         u_win.append(load_plane(users2, 2, "u2"))
@@ -79,12 +80,8 @@ def tile_attend_tab_twosum_changes_kernel(tc, keys_words, keys_scales, notes, mo
         u_win.append(load_plane(users2, 3, "u3"))
         l2 = load_list(offs2, "l2")
         n_win = [load_plane(notes, 0, "n0")]
-        load_scales(ms_win, more_scales, 0, 4)
-        load_scales(ms_win, more_scales, 1, 4)
-        n_win.append(load_plane(notes, 1, "n1"))
-        load_scales(ms_win, more_scales, 2, 4)
-        load_scales(ms_win, more_scales, 3, 4)
-        n_win += [load_plane(notes, t, "n%d" % t) for t in range(2, 4)]
+        n_win += [load_plane(notes, t, "n%d" % t) for t in range(1, 4)]
+        nc.sync.dma_start(mem_col[:], mem.rearrange("o (k c) -> (o k) c", c=4))
         nc.sync.dma_start(rowf_sb[:], rowf.rearrange("(p r) o -> p (r o)", r=4))
         kw_win = load_words(keys_words, "kw_win")
         v_win = [load_vals(b) for b in range(4)]
@@ -176,10 +173,9 @@ def tile_attend_tab_twosum_changes_kernel(tc, keys_words, keys_scales, notes, mo
         def shift(b, o):
             nc.vector.tensor_tensor(shifted[:, b, 1:J], o[:, 0 : J - 1], mem_row[:, 1:J], ALU.mult)
 
-        def finish(b, o):
-            res = sb([P, J], F32, "res%d" % b, {0: "vt2", 2: "vt3"}.get(b))
-            nc.vector.tensor_tensor(res[:], o[:], shifted[:, b, :], ALU.subtract)
-            nc.sync.dma_start(out[P * b : P * (b + 1), :], res[:])
+        def finish(b, o, res):
+            nc.vector.tensor_tensor(res, o[:], shifted[:, b, :], ALU.subtract)
+            nc.sync.dma_start(out[P * b : P * (b + 1), :], res)
 
         def last_block(b, vq):
             H = J // 2
@@ -197,7 +193,7 @@ def tile_attend_tab_twosum_changes_kernel(tc, keys_words, keys_scales, notes, mo
 
         mw = gather_words(mw_win, l3, "mw")
         gather_float("s", u_planes[:, 0, :], u_win[0], l4[:])
-        spread_mem()
+        ms = gather_scales(ms_win, l3, "ms")
         gather_float("v", u_planes[:, 1, :], u_win[1], l4[:])
         gather_float("s", u_planes[:, 2, :], u_win[2], l4[:])
         ks = gather_scales(ks_win, l1, "ks")
@@ -205,16 +201,16 @@ def tile_attend_tab_twosum_changes_kernel(tc, keys_words, keys_scales, notes, mo
         u_grp = sb([P, J, 4], BF16, "u_grp")
         weave(nc.vector.tensor_copy, u_grp, u_planes, 0, J)
         uq = quantize(u_grp, 0, J, "u")
-        ms = gather_scales(ms_win, l3, "ms")
         table_passes(mw, ms, 4, [(uq[0][:, 0:256], uq[1][:, 0:256]), (uq[0][:, 256:512], uq[1][:, 256:512])], True)
         for t in range(3):
             gather_float("s", n_planes[:, t, :], n_win[t], l2[:])
-        gather_float("s", n_planes[:, 3, 0:256], n_win[3], l2[:, 0:16])
-        gather_float("v", n_planes[:, 3, 256:512], n_win[3], l2[:, 16:32])
+        gather_float("s", n_planes[:, 3, 0:192], n_win[3], l2[:, 0:12])
+        gather_float("v", n_planes[:, 3, 192:512], n_win[3], l2[:, 12:32])
         n_grp = sb([P, J, 4], BF16, "n_grp")
         weave(nc.vector.tensor_copy, n_grp, n_planes, 0, 352)
         weave(nc.scalar.copy, n_grp, n_planes, 352, J)
         nq0 = quantize(n_grp, 0, 256, "na")
+        spread_mem()
         kw = gather_words(kw_win, l1, "kw")
         nq1 = quantize(n_grp, 256, J, "nb", "kw_win")
         table_passes(kw, ks, 0, [nq0, nq1], False)
@@ -228,8 +224,10 @@ def tile_attend_tab_twosum_changes_kernel(tc, keys_words, keys_scales, notes, mo
         prods = [product(b, vq[b]) for b in range(3)]
         shift(0, prods[0])
         shift(1, prods[1])
-        finish(0, prods[0])
-        finish(1, prods[1])
+        res01 = sb([P, 2, J], F32, "res01", "vt2")
+        finish(0, prods[0], res01[:, 0, :])
+        finish(1, prods[1], res01[:, 1, :])
         shift(2, prods[2])
-        finish(2, prods[2])
+        res2 = sb([P, J], F32, "res2", "vt3")
+        finish(2, prods[2], res2[:])
         last_block(3, vq[3])

@@ -14,8 +14,20 @@ ALU = mybir.AluOpType
 COPY = mybir.ActivationFunctionType.Copy
 
 P = 128
-D, T, I, J, U, X, Z, E = 512, 2048, 512, 512, 1024, 1024, 1024, 512
+PACK = 4
+D, T, I, J, E = 512, 2048, 512, 512, 512
 FLOPS = 2 * (2 * D * I * J + I * E * J)
+
+PER_COLUMN = 16
+QUADRANT = 32
+SCALE_ROWS = 16
+CHUNKS = J // P
+BLOCKS = E // P
+HALF = J // 2
+KEYS_FIRST, MORE_FIRST = 0, 4
+LAST_PLANE_ON_SCALAR = 192
+WEAVE_ON_VECTOR = 352
+TURN_BANKS = 4
 
 
 def tile_attend_tab_twosum_changes_kernel(tc, keys_words, keys_scales, notes, more_words, more_scales, users2,
@@ -26,208 +38,206 @@ def tile_attend_tab_twosum_changes_kernel(tc, keys_words, keys_scales, notes, mo
         keep = ctx.enter_context(tc.tile_pool(name="keep", bufs=1))
         psum = ctx.enter_context(tc.psum_pool(name="psum", bufs=1))
 
-        def sb(shape, dtype, name, tag=None):
-            return keep.tile(shape, dtype, name=name, tag=tag or name, align_bytes=64)
+        def sbuf(shape, dtype, name, after=None):
+            return keep.tile(shape, dtype, name=name, tag=after or name, align_bytes=64)
 
         def load_list(src, name):
-            t = lists.tile([P, 32], U16, name=name)
-            nc.sync.dma_start(t[:], src)
-            return t
+            tile = lists.tile([P, I // PER_COLUMN], U16, name=name)
+            nc.sync.dma_start(tile[:], src)
+            return tile
 
         def load_plane(src, t, name):
-            w = sb([P, src.shape[1]], F32, name)
-            nc.sync.dma_start(w[:], src.rearrange("(p t) u -> t p u", t=4)[t])
-            return w
+            window = sbuf([P, src.shape[1]], F32, name)
+            nc.sync.dma_start(window[:], src.rearrange("(p t) u -> t p u", t=PACK)[t])
+            return window
 
         def load_words(src, name):
-            w = sb([P, src.shape[2]], I32, name)
-            nc.sync.dma_start(w[:], src[0].rearrange("p n t -> p (n t)").bitcast(I32))
-            return w
+            window = sbuf([P, src.shape[2]], I32, name)
+            nc.sync.dma_start(window[:], src[0].rearrange("p n t -> p (n t)").bitcast(I32))
+            return window
 
-        def clear_scales(engine, src, name):
-            w = sb([P, src.shape[2]], U8, name)
-            engine.memset(w[:].bitcast(I32), 0)
-            return w
+        def cleared_scale_window(engine, src, name):
+            window = sbuf([P, src.shape[2]], U8, name)
+            engine.memset(window[:].bitcast(I32), 0)
+            return window
 
-        def load_scales(w, src, q, k):
-            nc.sync.dma_start(w[k + q : P : 32, :].bitcast(I32), src[0, q : 16 : 4, :].bitcast(I32))
+        def load_scales(window, src, first):
+            for m in range(PACK):
+                nc.sync.dma_start(window[first + m : P : QUADRANT, :].bitcast(I32),
+                                  src[0, m:SCALE_ROWS:PACK, :].bitcast(I32))
 
         def load_vals(b):
-            w = sb([P, T], F32, "vals%d" % b)
-            nc.sync.dma_start(w[:], vals[P * b : P * (b + 1), :])
-            return w
+            window = sbuf([P, T], F32, "vals%d" % b)
+            nc.sync.dma_start(window[:], vals[P * b : P * (b + 1), :])
+            return window
 
-        ms_win = clear_scales(nc.vector, more_scales, "ms_win")
-        ks_win = clear_scales(nc.gpsimd, keys_scales, "ks_win")
-        rowf_sb = sb([P, 4], F32, "rowf_sb")
-        mem_col = sb([P, 4], F32, "mem_col")
-        ident = sb([P, P], F32, "ident")
+        more_scales_win = cleared_scale_window(nc.vector, more_scales, "more_scales_win")
+        keys_scales_win = cleared_scale_window(nc.gpsimd, keys_scales, "keys_scales_win")
+        rowf_sb = sbuf([P, PACK], F32, "rowf_sb")
+        mem_cols = sbuf([P, PACK], F32, "mem_cols")
+        ident = sbuf([P, P], F32, "ident")
         make_identity(nc, ident[:])
-        shifted = sb([P, 4, J], F32, "shifted")
+        shifted = sbuf([P, BLOCKS, J], F32, "shifted")
         nc.vector.memset(shifted[:, :, 0:1], 0.0)
 
-        mw_win = load_words(more_words, "mw_win")
-        l3 = load_list(offs3, "l3")
-        u_win = [load_plane(users2, 0, "u0")]
-        l4 = load_list(offs4, "l4")
-        for q in range(4):
-            load_scales(ms_win, more_scales, q, 4)
-        u_win.append(load_plane(users2, 1, "u1"))
-        l1 = load_list(offs, "l1")
-        u_win.append(load_plane(users2, 2, "u2"))
-        for q in range(4):
-            load_scales(ks_win, keys_scales, q, 0)
-        u_win.append(load_plane(users2, 3, "u3"))
-        l2 = load_list(offs2, "l2")
-        n_win = [load_plane(notes, 0, "n0")]
-        n_win += [load_plane(notes, t, "n%d" % t) for t in range(1, 4)]
-        nc.sync.dma_start(mem_col[:], mem.rearrange("o (k c) -> (o k) c", c=4))
-        nc.sync.dma_start(rowf_sb[:], rowf.rearrange("(p r) o -> p (r o)", r=4))
-        kw_win = load_words(keys_words, "kw_win")
-        v_win = [load_vals(b) for b in range(4)]
+        idx3 = load_list(offs3, "idx3")
+        more_words_win = load_words(more_words, "more_words_win")
+        idx4 = load_list(offs4, "idx4")
+        users_win = [load_plane(users2, 0, "users0")]
+        load_scales(more_scales_win, more_scales, MORE_FIRST)
+        users_win.append(load_plane(users2, 1, "users1"))
+        idx = load_list(offs, "idx")
+        users_win.append(load_plane(users2, 2, "users2"))
+        load_scales(keys_scales_win, keys_scales, KEYS_FIRST)
+        users_win.append(load_plane(users2, 3, "users3"))
+        idx2 = load_list(offs2, "idx2")
+        notes_win = [load_plane(notes, t, "notes%d" % t) for t in range(PACK)]
+        nc.sync.dma_start(mem_cols[:], mem.rearrange("o (k c) -> (o k) c", c=PACK))
+        nc.sync.dma_start(rowf_sb[:], rowf.rearrange("(s r) o -> s (r o)", r=PACK))
+        keys_words_win = load_words(keys_words, "keys_words_win")
+        vals_win = [load_vals(b) for b in range(BLOCKS)]
 
-        def gather_float(engine, dst, win, lst):
-            if engine == "v":
-                nc.vector.tensor_copy(dst, win[:].indirect(lst))
-            else:
-                nc.scalar.activation(dst, win[:].indirect(lst), COPY)
+        def entries(listed, n0, n1):
+            return listed[:, n0 // PER_COLUMN : n1 // PER_COLUMN]
 
-        def dealt(t):
-            return t[:].rearrange("p r s -> p s r")
+        def vector_gather(dst, window, offsets):
+            nc.vector.tensor_copy(dst, window[:].indirect(offsets))
 
-        def gather_words(win, lst, name):
-            g = sb([P, 4, P], U32, name)
-            nc.vector.tensor_copy(dealt(g), win[:].bitcast(U32).indirect(lst[:]))
-            return g
+        def scalar_gather(dst, window, offsets):
+            nc.scalar.activation(dst, window[:].indirect(offsets), COPY)
 
-        def gather_scales(win, lst, name):
-            g = sb([P, 4, P], U8, name)
-            nc.vector.tensor_copy(dealt(g), win[:].indirect(lst[:]))
-            return g
+        def gather_dealt(window, dtype, listed, name):
+            dealt = sbuf([P, PACK, P], dtype, name)
+            nc.vector.tensor_copy(dealt[:].rearrange("p r s -> p s r"), window.indirect(listed[:]))
+            return dealt
 
-        def weave(copy, g, planes, c0, c1):
-            copy(g[:, c0:c1, :].rearrange("p (c i) t -> p c t i", i=4), planes[:, :, c0:c1].rearrange("p t (c i) -> p c t i", i=4))
+        def weave(copy, woven, planes, c0, c1):
+            copy(woven[:, c0:c1, :].rearrange("p (c n) t -> p c t n", n=PACK),
+                 planes[:, :, c0:c1].rearrange("p t (c n) -> p c t n", n=PACK))
 
-        def quantize(g, c0, c1, name, tag=None):
-            codes = sb([P, c1 - c0], U32, name + "_codes", tag)
-            scales = sb([P, c1 - c0], U8, name + "_scales")
-            nc.vector.quantize_mx(out=codes[:].bitcast(FP8X4), scales=scales[:], in_=g[:, c0:c1, :].rearrange("p w t -> p (w t)"))
-            return codes, scales
+        def quantize_into(codes, scales, woven):
+            nc.vector.quantize_mx(out=codes.bitcast(FP8X4), scales=scales, in_=woven.rearrange("p w t -> p (w t)"))
 
-        n_planes = sb([P, 4, J], BF16, "n_planes")
-        u_planes = sb([P, 4, J], BF16, "u_planes")
-        banks = [psum.tile([P, 4, P], F32, name="table%d" % c) for c in range(4)]
+        def quantize(woven, c0, c1, name, after=None):
+            codes = sbuf([P, c1 - c0], U32, name + "_codes", after)
+            scales = sbuf([P, c1 - c0], U8, name + "_scales")
+            quantize_into(codes[:], scales[:], woven[:, c0:c1, :])
+            return codes[:], scales[:]
 
-        def table_passes(words, scales, k, halves, first):
-            for c in range(4):
-                codes, cscales = halves[c // 2]
-                cols = slice(P * (c % 2), P * (c % 2 + 1))
-                for r in range(4):
-                    nc.tensor.matmul_mx(out=banks[c][:, r, :], lhsT=words[:, r, :].bitcast(FP8X4), lhsT_scale=scales[k:P, r, :],
-                                        rhs=codes[:, cols].bitcast(FP8X4), rhs_scale=cscales[:, cols],
-                                        start=(first and r == 0), stop=(not first and r == 3))
+        notes_planes = sbuf([P, PACK, J], BF16, "notes_planes")
+        users_planes = sbuf([P, PACK, J], BF16, "users_planes")
+        table_banks = [psum.tile([P, PACK, P], F32, name="table%d" % c) for c in range(CHUNKS)]
 
-        mem_row = sb([P, J], F32, "mem_row")
+        def table_passes(words, scales, first, halves, opens):
+            for c in range(CHUNKS):
+                codes, code_scales = halves[P * c // HALF]
+                cols = slice(P * c % HALF, P * c % HALF + P)
+                for r in range(PACK):
+                    nc.tensor.matmul_mx(out=table_banks[c][:, r, :],
+                                        lhsT=words[:, r, :].bitcast(FP8X4), lhsT_scale=scales[first:P, r, :],
+                                        rhs=codes[:, cols].bitcast(FP8X4), rhs_scale=code_scales[:, cols],
+                                        start=(opens and r == 0), stop=(not opens and r == PACK - 1))
 
-        def spread_mem():
-            bank = psum.tile([P, 4, P], F32, name="turn", bufs=4)
-            for c in range(4):
-                nc.tensor.transpose(bank[:, c, :], mem_col[:, c : c + 1].to_broadcast([P, P]), ident[:])
-            nc.scalar.copy(mem_row[:].rearrange("p (k c) -> p k c", c=4), bank[:].rearrange("p c k -> p k c"))
+        more_dealt = gather_dealt(more_words_win[:].bitcast(U32), U32, idx3, "more_dealt")
+        scalar_gather(users_planes[:, 0, :], users_win[0], idx4[:])
+        more_scales_dealt = gather_dealt(more_scales_win[:], U8, idx3, "more_scales_dealt")
+        vector_gather(users_planes[:, 1, :], users_win[1], idx4[:])
+        scalar_gather(users_planes[:, 2, :], users_win[2], idx4[:])
+        keys_scales_dealt = gather_dealt(keys_scales_win[:], U8, idx, "keys_scales_dealt")
+        vector_gather(users_planes[:, 3, :], users_win[3], idx4[:])
+        users_woven = sbuf([P, J, PACK], BF16, "users_woven")
+        weave(nc.vector.tensor_copy, users_woven, users_planes, 0, J)
+        users_codes, users_scales = quantize(users_woven, 0, J, "users")
+        users_halves = [(users_codes[:, c0 : c0 + HALF], users_scales[:, c0 : c0 + HALF]) for c0 in (0, HALF)]
+        table_passes(more_dealt, more_scales_dealt, MORE_FIRST, users_halves, True)
 
-        gr = sb([P, J, 4], BF16, "gr")
-        gr_codes = sb([P, J], U32, "gr_codes")
-        gr_scales = sb([P, J], U8, "gr_scales")
-        rowf_b = rowf_sb[:].rearrange("p (o r) -> p o r", o=1).to_broadcast([P, P, 4])
+        last = PACK - 1
+        for t in range(last):
+            scalar_gather(notes_planes[:, t, :], notes_win[t], idx2[:])
+        scalar_gather(notes_planes[:, last, 0:LAST_PLANE_ON_SCALAR], notes_win[last], entries(idx2, 0, LAST_PLANE_ON_SCALAR))
+        vector_gather(notes_planes[:, last, LAST_PLANE_ON_SCALAR:J], notes_win[last], entries(idx2, LAST_PLANE_ON_SCALAR, J))
+        notes_woven = sbuf([P, J, PACK], BF16, "notes_woven")
+        weave(nc.vector.tensor_copy, notes_woven, notes_planes, 0, WEAVE_ON_VECTOR)
+        weave(nc.scalar.copy, notes_woven, notes_planes, WEAVE_ON_VECTOR, J)
+        notes_low = quantize(notes_woven, 0, HALF, "notes_low")
 
-        def table_out(c):
-            nc.vector.scalar_tensor_tensor(gr[:, P * c : P * (c + 1), :], banks[c][:].rearrange("p r n -> p n r"), 0.0, rowf_b, ALU.max, ALU.mult)
+        mem_row = sbuf([P, J], F32, "mem_row")
+        mem_bank = psum.tile([P, PACK, P], F32, name="turn", bufs=TURN_BANKS)
+        for c in range(PACK):
+            nc.tensor.transpose(mem_bank[:, c, :], mem_cols[:, c : c + 1].to_broadcast([P, P]), ident[:])
+        nc.scalar.copy(mem_row[:].rearrange("p (k c) -> p k c", c=PACK), mem_bank[:].rearrange("p c k -> p k c"))
 
-        def table_quant(c0, c1):
-            cols = slice(P * c0, P * c1)
-            nc.vector.quantize_mx(out=gr_codes[:, cols].bitcast(FP8X4), scales=gr_scales[:, cols], in_=gr[:, cols, :].rearrange("p w t -> p (w t)"))
+        keys_dealt = gather_dealt(keys_words_win[:].bitcast(U32), U32, idx, "keys_dealt")
+        notes_high = quantize(notes_woven, HALF, J, "notes_high", after="keys_words_win")
+        table_passes(keys_dealt, keys_scales_dealt, KEYS_FIRST, [notes_low, notes_high], False)
 
-        def vals_gather(b, split):
-            g = sb([P, I], BF16, "vg%d" % b)
-            if split:
-                gather_float("s", g[:, 0:split], v_win[b], l1[:, 0 : split // 16])
-                gather_float("v", g[:, split:I], v_win[b], l1[:, split // 16 : I // 16])
-            else:
-                gather_float("s", g[:], v_win[b], l1[:])
-            return g
+        vals_picked = []
+        for b in range(BLOCKS):
+            picked = sbuf([P, I], BF16, "vals_picked%d" % b)
+            scalar_gather(picked[:], vals_win[b], idx[:])
+            vals_picked.append(picked)
 
-        def vals_turn(b, g):
-            words = g[:].bitcast(F32)
-            bank = psum.tile([P, 4, P], F32, name="turn", bufs=4)
+        gr1 = sbuf([P, J, PACK], BF16, "gr1")
+        gr1_codes = sbuf([P, J], U32, "gr1_codes")
+        gr1_scales = sbuf([P, J], U8, "gr1_scales")
+        rowf_wide = rowf_sb[:].rearrange("p (o r) -> p o r", o=1).to_broadcast([P, P, PACK])
+
+        def empty_table_bank(c):
+            nc.vector.scalar_tensor_tensor(gr1[:, P * c : P * (c + 1), :], table_banks[c][:].rearrange("p r n -> p n r"),
+                                           0.0, rowf_wide, ALU.max, ALU.mult)
+
+        for c in range(CHUNKS - 1):
+            empty_table_bank(c)
+        quantize_into(gr1_codes[:, 0:HALF], gr1_scales[:, 0:HALF], gr1[:, 0:HALF, :])
+        empty_table_bank(CHUNKS - 1)
+        quantize_into(gr1_codes[:, HALF:J], gr1_scales[:, HALF:J], gr1[:, HALF:J, :])
+
+        def turn_vals(b, after):
+            words = vals_picked[b][:].bitcast(F32)
+            bank = psum.tile([P, PACK, P], F32, name="turn", bufs=TURN_BANKS)
             for u in range(2):
                 nc.tensor.transpose(bank[:, u, :], words[:, u : 2 * P : 2], ident[:])
-            vt = sb([P, P, 4], BF16, "vt%d" % b, "vals1" if b == 0 else None)
-            nc.scalar.copy(vt[:].bitcast(F32), bank[:, 0:2, :].rearrange("p u e -> p e u"))
-            return vt
+            turned = sbuf([P, P, PACK], BF16, "turned%d" % b, after)
+            nc.scalar.copy(turned[:].bitcast(F32), bank[:, 0:2, :].rearrange("p u e -> p e u"))
+            return turned
 
-        def product(b, vq):
+        turned_after = {1: "vals2"}
+        vt1 = [quantize(turn_vals(b, turned_after.get(b)), 0, P, "vt1_%d" % b) for b in range(BLOCKS)]
+
+        def product(o, b, cols):
+            codes, scales = vt1[b]
+            nc.tensor.matmul_mx(out=o[:], lhsT=codes.bitcast(FP8X4), lhsT_scale=scales,
+                                rhs=gr1_codes[:, cols].bitcast(FP8X4), rhs_scale=gr1_scales[:, cols], start=True, stop=True)
+
+        def shift(b, j0, j1, o_before):
+            nc.vector.tensor_tensor(shifted[:, b, j0:j1], o_before, mem_row[:, j0:j1], ALU.mult)
+
+        def subtract_and_store(b, cols, o, result):
+            nc.vector.tensor_tensor(result, o[:], shifted[:, b, cols], ALU.subtract)
+            nc.sync.dma_start(out[P * b : P * (b + 1), cols], result)
+
+        whole = slice(0, J)
+        final = BLOCKS - 1
+        sums = []
+        for b in range(final):
             o = psum.tile([P, J], F32, name="table%d" % b)
-            nc.tensor.matmul_mx(out=o[:], lhsT=vq[0][:].bitcast(FP8X4), lhsT_scale=vq[1][:], rhs=gr_codes[:].bitcast(FP8X4), rhs_scale=gr_scales[:], start=True, stop=True)
-            return o
+            product(o, b, whole)
+            sums.append(o)
+        results = sbuf([P, final - 1, J], F32, "results")
+        for b in range(final - 1):
+            shift(b, 1, J, sums[b][:, 0 : J - 1])
+            subtract_and_store(b, whole, sums[b], results[:, b, :])
+        shift(final - 1, 1, J, sums[final - 1][:, 0 : J - 1])
+        late_result = sbuf([P, J], F32, "late_result", after="turned%d" % final)
+        subtract_and_store(final - 1, whole, sums[final - 1], late_result[:])
 
-        def shift(b, o):
-            nc.vector.tensor_tensor(shifted[:, b, 1:J], o[:, 0 : J - 1], mem_row[:, 1:J], ALU.mult)
-
-        def finish(b, o, res):
-            nc.vector.tensor_tensor(res, o[:], shifted[:, b, :], ALU.subtract)
-            nc.sync.dma_start(out[P * b : P * (b + 1), :], res)
-
-        def last_block(b, vq):
-            H = J // 2
-            o = [psum.tile([P, H], F32, name="table3"), psum.tile([P, H], F32, name="turn", bufs=4)]
-            for h in range(2):
-                cols = slice(H * h, H * (h + 1))
-                nc.tensor.matmul_mx(out=o[h][:], lhsT=vq[0][:].bitcast(FP8X4), lhsT_scale=vq[1][:], rhs=gr_codes[:, cols].bitcast(FP8X4), rhs_scale=gr_scales[:, cols], start=True, stop=True)
-            nc.vector.tensor_tensor(shifted[:, b, 1 : H + 1], o[0][:], mem_row[:, 1 : H + 1], ALU.mult)
-            nc.vector.tensor_tensor(shifted[:, b, H + 1 : J], o[1][:, 0 : H - 1], mem_row[:, H + 1 : J], ALU.mult)
-            for h in range(2):
-                cols = slice(H * h, H * (h + 1))
-                res = sb([P, H], F32, "last%d" % h)
-                nc.vector.tensor_tensor(res[:], o[h][:], shifted[:, b, cols], ALU.subtract)
-                nc.sync.dma_start(out[P * b : P * (b + 1), cols], res[:])
-
-        mw = gather_words(mw_win, l3, "mw")
-        gather_float("s", u_planes[:, 0, :], u_win[0], l4[:])
-        ms = gather_scales(ms_win, l3, "ms")
-        gather_float("v", u_planes[:, 1, :], u_win[1], l4[:])
-        gather_float("s", u_planes[:, 2, :], u_win[2], l4[:])
-        ks = gather_scales(ks_win, l1, "ks")
-        gather_float("v", u_planes[:, 3, :], u_win[3], l4[:])
-        u_grp = sb([P, J, 4], BF16, "u_grp")
-        weave(nc.vector.tensor_copy, u_grp, u_planes, 0, J)
-        uq = quantize(u_grp, 0, J, "u")
-        table_passes(mw, ms, 4, [(uq[0][:, 0:256], uq[1][:, 0:256]), (uq[0][:, 256:512], uq[1][:, 256:512])], True)
-        for t in range(3):
-            gather_float("s", n_planes[:, t, :], n_win[t], l2[:])
-        gather_float("s", n_planes[:, 3, 0:192], n_win[3], l2[:, 0:12])
-        gather_float("v", n_planes[:, 3, 192:512], n_win[3], l2[:, 12:32])
-        n_grp = sb([P, J, 4], BF16, "n_grp")
-        weave(nc.vector.tensor_copy, n_grp, n_planes, 0, 352)
-        weave(nc.scalar.copy, n_grp, n_planes, 352, J)
-        nq0 = quantize(n_grp, 0, 256, "na")
-        spread_mem()
-        kw = gather_words(kw_win, l1, "kw")
-        nq1 = quantize(n_grp, 256, J, "nb", "kw_win")
-        table_passes(kw, ks, 0, [nq0, nq1], False)
-        vg = [vals_gather(b, 0) for b in range(4)]
-        for c in range(3):
-            table_out(c)
-        table_quant(0, 2)
-        table_out(3)
-        table_quant(2, 4)
-        vq = [quantize(vals_turn(b, vg[b]), 0, P, "v%d" % b) for b in range(4)]
-        prods = [product(b, vq[b]) for b in range(3)]
-        shift(0, prods[0])
-        shift(1, prods[1])
-        res01 = sb([P, 2, J], F32, "res01", "vt2")
-        finish(0, prods[0], res01[:, 0, :])
-        finish(1, prods[1], res01[:, 1, :])
-        shift(2, prods[2])
-        res2 = sb([P, J], F32, "res2", "vt3")
-        finish(2, prods[2], res2[:])
-        last_block(3, vq[3])
+        o_low = psum.tile([P, HALF], F32, name="table%d" % final)
+        o_high = psum.tile([P, HALF], F32, name="turn", bufs=TURN_BANKS)
+        low, high = slice(0, HALF), slice(HALF, J)
+        product(o_low, final, low)
+        product(o_high, final, high)
+        shift(final, 1, HALF + 1, o_low[:])
+        shift(final, HALF + 1, J, o_high[:, 0 : HALF - 1])
+        for name, cols, o in (("result_low", low, o_low), ("result_high", high, o_high)):
+            result = sbuf([P, HALF], F32, name)
+            subtract_and_store(final, cols, o, result[:])

from contextlib import ExitStack

import concourse.mybir as mybir
from concourse.masks import make_identity

F32 = mybir.dt.float32
BF16 = mybir.dt.bfloat16
I32 = mybir.dt.int32
U32 = mybir.dt.uint32
U16 = mybir.dt.uint16
U8 = mybir.dt.uint8
FP8X4 = mybir.dt.float8_e4m3fn_x4
ALU = mybir.AluOpType
COPY = mybir.ActivationFunctionType.Copy

P = 128
PACK = 4
D, T, I, J, E = 512, 2048, 512, 512, 512
FLOPS = 2 * (2 * D * I * J + I * E * J)

PER_COLUMN = 16
QUADRANT = 32
SCALE_ROWS = 16
CHUNKS = J // P
BLOCKS = E // P
HALF = J // 2
KEYS_FIRST, MORE_FIRST = 0, 4
LAST_PLANE_ON_SCALAR = 192
WEAVE_ON_VECTOR = 352
TURN_BANKS = 4


def tile_attend_tab_twosum_changes_kernel(tc, keys_words, keys_scales, notes, more_words, more_scales, users2,
                                           rowf, vals, mem, offs, offs2, offs3, offs4, out):
    nc = tc.nc
    with ExitStack() as ctx:
        lists = ctx.enter_context(tc.tile_pool(name="lists", bufs=1))
        keep = ctx.enter_context(tc.tile_pool(name="keep", bufs=1))
        psum = ctx.enter_context(tc.psum_pool(name="psum", bufs=1))

        def sbuf(shape, dtype, name, after=None):
            return keep.tile(shape, dtype, name=name, tag=after or name, align_bytes=64)

        def load_list(src, name):
            tile = lists.tile([P, I // PER_COLUMN], U16, name=name)
            nc.sync.dma_start(tile[:], src)
            return tile

        def load_plane(src, t, name):
            window = sbuf([P, src.shape[1]], F32, name)
            nc.sync.dma_start(window[:], src.rearrange("(p t) u -> t p u", t=PACK)[t])
            return window

        def load_words(src, name):
            window = sbuf([P, src.shape[2]], I32, name)
            nc.sync.dma_start(window[:], src[0].rearrange("p n t -> p (n t)").bitcast(I32))
            return window

        def cleared_scale_window(engine, src, name):
            window = sbuf([P, src.shape[2]], U8, name)
            engine.memset(window[:].bitcast(I32), 0)
            return window

        def load_scales(window, src, first):
            for m in range(PACK):
                nc.sync.dma_start(window[first + m : P : QUADRANT, :].bitcast(I32),
                                  src[0, m:SCALE_ROWS:PACK, :].bitcast(I32))

        def load_vals(b):
            window = sbuf([P, T], F32, "vals%d" % b)
            nc.sync.dma_start(window[:], vals[P * b : P * (b + 1), :])
            return window

        more_scales_win = cleared_scale_window(nc.vector, more_scales, "more_scales_win")
        keys_scales_win = cleared_scale_window(nc.gpsimd, keys_scales, "keys_scales_win")
        rowf_sb = sbuf([P, PACK], F32, "rowf_sb")
        mem_cols = sbuf([P, PACK], F32, "mem_cols")
        ident = sbuf([P, P], F32, "ident")
        make_identity(nc, ident[:])
        shifted = sbuf([P, BLOCKS, J], F32, "shifted")
        nc.vector.memset(shifted[:, :, 0:1], 0.0)

        idx3 = load_list(offs3, "idx3")
        more_words_win = load_words(more_words, "more_words_win")
        idx4 = load_list(offs4, "idx4")
        users_win = [load_plane(users2, 0, "users0")]
        load_scales(more_scales_win, more_scales, MORE_FIRST)
        users_win.append(load_plane(users2, 1, "users1"))
        idx = load_list(offs, "idx")
        users_win.append(load_plane(users2, 2, "users2"))
        load_scales(keys_scales_win, keys_scales, KEYS_FIRST)
        users_win.append(load_plane(users2, 3, "users3"))
        idx2 = load_list(offs2, "idx2")
        notes_win = [load_plane(notes, t, "notes%d" % t) for t in range(PACK)]
        nc.sync.dma_start(mem_cols[:], mem.rearrange("o (k c) -> (o k) c", c=PACK))
        nc.sync.dma_start(rowf_sb[:], rowf.rearrange("(s r) o -> s (r o)", r=PACK))
        keys_words_win = load_words(keys_words, "keys_words_win")
        vals_win = [load_vals(b) for b in range(BLOCKS)]

        def entries(listed, n0, n1):
            return listed[:, n0 // PER_COLUMN : n1 // PER_COLUMN]

        def vector_gather(dst, window, offsets):
            nc.vector.tensor_copy(dst, window[:].indirect(offsets))

        def scalar_gather(dst, window, offsets):
            nc.scalar.activation(dst, window[:].indirect(offsets), COPY)

        def gather_dealt(window, dtype, listed, name):
            dealt = sbuf([P, PACK, P], dtype, name)
            nc.vector.tensor_copy(dealt[:].rearrange("p r s -> p s r"), window.indirect(listed[:]))
            return dealt

        def weave(copy, woven, planes, c0, c1):
            copy(woven[:, c0:c1, :].rearrange("p (c n) t -> p c t n", n=PACK),
                 planes[:, :, c0:c1].rearrange("p t (c n) -> p c t n", n=PACK))

        def quantize_into(codes, scales, woven):
            nc.vector.quantize_mx(out=codes.bitcast(FP8X4), scales=scales, in_=woven.rearrange("p w t -> p (w t)"))

        def quantize(woven, c0, c1, name, after=None):
            codes = sbuf([P, c1 - c0], U32, name + "_codes", after)
            scales = sbuf([P, c1 - c0], U8, name + "_scales")
            quantize_into(codes[:], scales[:], woven[:, c0:c1, :])
            return codes[:], scales[:]

        notes_planes = sbuf([P, PACK, J], BF16, "notes_planes")
        users_planes = sbuf([P, PACK, J], BF16, "users_planes")
        table_banks = [psum.tile([P, PACK, P], F32, name="table%d" % c) for c in range(CHUNKS)]

        def table_passes(words, scales, first, halves, opens):
            for c in range(CHUNKS):
                codes, code_scales = halves[P * c // HALF]
                cols = slice(P * c % HALF, P * c % HALF + P)
                for r in range(PACK):
                    nc.tensor.matmul_mx(out=table_banks[c][:, r, :],
                                        lhsT=words[:, r, :].bitcast(FP8X4), lhsT_scale=scales[first:P, r, :],
                                        rhs=codes[:, cols].bitcast(FP8X4), rhs_scale=code_scales[:, cols],
                                        start=(opens and r == 0), stop=(not opens and r == PACK - 1))

        more_dealt = gather_dealt(more_words_win[:].bitcast(U32), U32, idx3, "more_dealt")
        scalar_gather(users_planes[:, 0, :], users_win[0], idx4[:])
        more_scales_dealt = gather_dealt(more_scales_win[:], U8, idx3, "more_scales_dealt")
        vector_gather(users_planes[:, 1, :], users_win[1], idx4[:])
        scalar_gather(users_planes[:, 2, :], users_win[2], idx4[:])
        keys_scales_dealt = gather_dealt(keys_scales_win[:], U8, idx, "keys_scales_dealt")
        vector_gather(users_planes[:, 3, :], users_win[3], idx4[:])
        users_woven = sbuf([P, J, PACK], BF16, "users_woven")
        weave(nc.vector.tensor_copy, users_woven, users_planes, 0, J)
        users_codes, users_scales = quantize(users_woven, 0, J, "users")
        users_halves = [(users_codes[:, c0 : c0 + HALF], users_scales[:, c0 : c0 + HALF]) for c0 in (0, HALF)]
        table_passes(more_dealt, more_scales_dealt, MORE_FIRST, users_halves, True)

        last = PACK - 1
        for t in range(last):
            scalar_gather(notes_planes[:, t, :], notes_win[t], idx2[:])
        scalar_gather(notes_planes[:, last, 0:LAST_PLANE_ON_SCALAR], notes_win[last], entries(idx2, 0, LAST_PLANE_ON_SCALAR))
        vector_gather(notes_planes[:, last, LAST_PLANE_ON_SCALAR:J], notes_win[last], entries(idx2, LAST_PLANE_ON_SCALAR, J))
        notes_woven = sbuf([P, J, PACK], BF16, "notes_woven")
        weave(nc.vector.tensor_copy, notes_woven, notes_planes, 0, WEAVE_ON_VECTOR)
        weave(nc.scalar.copy, notes_woven, notes_planes, WEAVE_ON_VECTOR, J)
        notes_low = quantize(notes_woven, 0, HALF, "notes_low")

        mem_row = sbuf([P, J], F32, "mem_row")
        mem_bank = psum.tile([P, PACK, P], F32, name="turn", bufs=TURN_BANKS)
        for c in range(PACK):
            nc.tensor.transpose(mem_bank[:, c, :], mem_cols[:, c : c + 1].to_broadcast([P, P]), ident[:])
        nc.scalar.copy(mem_row[:].rearrange("p (k c) -> p k c", c=PACK), mem_bank[:].rearrange("p c k -> p k c"))

        keys_dealt = gather_dealt(keys_words_win[:].bitcast(U32), U32, idx, "keys_dealt")
        notes_high = quantize(notes_woven, HALF, J, "notes_high", after="keys_words_win")
        table_passes(keys_dealt, keys_scales_dealt, KEYS_FIRST, [notes_low, notes_high], False)

        vals_picked = []
        for b in range(BLOCKS):
            picked = sbuf([P, I], BF16, "vals_picked%d" % b)
            scalar_gather(picked[:], vals_win[b], idx[:])
            vals_picked.append(picked)

        gr1 = sbuf([P, J, PACK], BF16, "gr1")
        gr1_codes = sbuf([P, J], U32, "gr1_codes")
        gr1_scales = sbuf([P, J], U8, "gr1_scales")
        rowf_wide = rowf_sb[:].rearrange("p (o r) -> p o r", o=1).to_broadcast([P, P, PACK])

        def empty_table_bank(c):
            nc.vector.scalar_tensor_tensor(gr1[:, P * c : P * (c + 1), :], table_banks[c][:].rearrange("p r n -> p n r"),
                                           0.0, rowf_wide, ALU.max, ALU.mult)

        for c in range(CHUNKS - 1):
            empty_table_bank(c)
        quantize_into(gr1_codes[:, 0:HALF], gr1_scales[:, 0:HALF], gr1[:, 0:HALF, :])
        empty_table_bank(CHUNKS - 1)
        quantize_into(gr1_codes[:, HALF:J], gr1_scales[:, HALF:J], gr1[:, HALF:J, :])

        def turn_vals(b, after):
            words = vals_picked[b][:].bitcast(F32)
            bank = psum.tile([P, PACK, P], F32, name="turn", bufs=TURN_BANKS)
            for u in range(2):
                nc.tensor.transpose(bank[:, u, :], words[:, u : 2 * P : 2], ident[:])
            turned = sbuf([P, P, PACK], BF16, "turned%d" % b, after)
            nc.scalar.copy(turned[:].bitcast(F32), bank[:, 0:2, :].rearrange("p u e -> p e u"))
            return turned

        turned_after = {1: "vals2"}
        vt1 = [quantize(turn_vals(b, turned_after.get(b)), 0, P, "vt1_%d" % b) for b in range(BLOCKS)]

        def product(o, b, cols):
            codes, scales = vt1[b]
            nc.tensor.matmul_mx(out=o[:], lhsT=codes.bitcast(FP8X4), lhsT_scale=scales,
                                rhs=gr1_codes[:, cols].bitcast(FP8X4), rhs_scale=gr1_scales[:, cols], start=True, stop=True)

        def shift(b, j0, j1, o_before):
            nc.vector.tensor_tensor(shifted[:, b, j0:j1], o_before, mem_row[:, j0:j1], ALU.mult)

        def subtract_and_store(b, cols, o, result):
            nc.vector.tensor_tensor(result, o[:], shifted[:, b, cols], ALU.subtract)
            nc.sync.dma_start(out[P * b : P * (b + 1), cols], result)

        whole = slice(0, J)
        final = BLOCKS - 1
        sums = []
        for b in range(final):
            o = psum.tile([P, J], F32, name="table%d" % b)
            product(o, b, whole)
            sums.append(o)
        results = sbuf([P, final - 1, J], F32, "results")
        for b in range(final - 1):
            shift(b, 1, J, sums[b][:, 0 : J - 1])
            subtract_and_store(b, whole, sums[b], results[:, b, :])
        shift(final - 1, 1, J, sums[final - 1][:, 0 : J - 1])
        late_result = sbuf([P, J], F32, "late_result", after="turned%d" % final)
        subtract_and_store(final - 1, whole, sums[final - 1], late_result[:])

        o_low = psum.tile([P, HALF], F32, name="table%d" % final)
        o_high = psum.tile([P, HALF], F32, name="turn", bufs=TURN_BANKS)
        low, high = slice(0, HALF), slice(HALF, J)
        product(o_low, final, low)
        product(o_high, final, high)
        shift(final, 1, HALF + 1, o_low[:])
        shift(final, HALF + 1, J, o_high[:, 0 : HALF - 1])
        for name, cols, o in (("result_low", low, o_low), ("result_high", high, o_high)):
            result = sbuf([P, HALF], F32, name)
            subtract_and_store(final, cols, o, result[:])
